import numpy as np, ml_dtypes
CORES = [2,7,18,23,34]
N = 5
import mx_ref
BF = ml_dtypes.bfloat16
def gentries(a):
    return np.ascontiguousarray(a.reshape(8, 16, -1).transpose(0, 2, 1)).reshape(8, -1)
def gtable(e):
    e = np.asarray(e); return np.ascontiguousarray(e.reshape(8, -1, 16).transpose(0, 2, 1)).reshape(128, -1).astype(np.int32)
def gcols(t, e):
    v = np.concatenate([t.reshape(8, 16, -1, 4), np.zeros((8, 16, 1, 4), BF)], axis=2)
    return np.ascontiguousarray(np.stack([v[g][:, e[g]] for g in range(8)])).reshape(128, -1)
def f(rng, *shape):
    return mx_ref.flush((rng.standard_normal(shape, dtype=np.float32) * np.exp2(rng.integers(-2, 3, shape[:-1] + (1,)))).astype(BF))
def wide(rng, *shape, cols=0):
    v = rng.standard_normal(shape, dtype=np.float32) * np.exp2(rng.integers(-12, 13, shape)).astype(np.float32)
    if cols: v *= np.repeat(np.exp2(rng.integers(-cols, cols + 1, shape[:-2] + (1, shape[-1] // 4))) * (rng.random(shape[:-2] + (1, shape[-1] // 4)) > 0.0625), 4, axis=-1).astype(np.float32)
    return mx_ref.flush(v.astype(BF))
T, O, K = 128, 4, 256
def lists(rng, alike=False, groups=False, ends=False, few=False):
    c = []
    for r in range(N):
        e = rng.integers(0, K, (8, O, 2, 128))
        if groups: e = np.stack([e[0]] * 8)
        if ends: e = rng.permuted(np.resize([0, K - 1], (8, O, 2, 128)), axis=3)
        if few:
            for m in range(2): e[:, :, m] = rng.permutation(np.resize(rng.permutation(K)[:8], 8 * O * 128)).reshape(8, O, 128)
        c.append(gtable(e.reshape(8, -1)))
    if alike: c = [c[0]] * N
    return np.stack(c)
def setup_inputs(rng):
    return {"x": f(rng, N, 128, 4 * T), "book": np.stack([f(rng, 128, 8 * K)] * N), "cw": lists(rng)}
def setup_inputs_alike(rng):
    d = setup_inputs(rng); d["cw"] = lists(rng, alike=True); return d
def setup_inputs_groups(rng):
    d = setup_inputs(rng); d["cw"] = lists(rng, groups=True); return d
def setup_inputs_ends(rng):
    d = setup_inputs(rng); d["cw"] = lists(rng, ends=True); return d
def setup_inputs_few(rng):
    d = setup_inputs(rng); d["cw"] = lists(rng, few=True); return d
def setup_inputs_spread(rng):
    d = setup_inputs(rng); d["x"] = wide(rng, N, 128, 4 * T, cols=8); d["book"] = np.stack([wide(rng, 128, 8 * K, cols=4)] * N); return d
def check_inputs(d):
    b = []
    for r in range(N):
        if d["cw"][r].min() < 0 or d["cw"][r].max() >= K: b.append("cw")
        if d["book"][r].tobytes() != d["book"][0].tobytes(): b.append("book")
    return b
def reference(x, book, cw):
    W = []
    for s in range(N):
        e = gentries(cw[s])
        for o in range(O):
            a, b = [gcols(np.ascontiguousarray(book[s][:, 4 * K * m:4 * K * m + 4 * K]), e[:, (2 * o + m) * 128:(2 * o + m) * 128 + 128]).astype(np.float32) for m in range(2)]
            W.append(mx_ref.quantize((a + b).astype(BF)))
    y = np.zeros((N, 128, N * O * T), np.float32)
    for r in range(N):
        X = mx_ref.quantize(np.ascontiguousarray(x[r]))
        for i in range(N * O): y[r][:, T * i:T * i + T] = mx_ref.matmul(W[i], X)
    return {"y": y}

from concourse.bass import DstId, RemoteDMATransfer
from concourse.mybir import dt, AluOpType, ActivationFunctionType

NR, O, TC = 5, 4, 128
NB = 2 * NR
BC = 2 * TC
LC = 2 * BC // 16

MAKE = [[0, 1, 5, 9], [2, 3, 7, 9], [4, 5, 1, 9], [6, 7, 3, 9], [8, 9, 3, 5]]
SEND = [
    {0: [1, 2, 3, 4], 1: [1, 4], 5: [1]},
    {2: [0, 2, 3, 4], 3: [0], 7: [0]},
    {4: [3, 0, 1, 4], 5: [3], 1: [3]},
    {6: [2, 0, 1, 4], 7: [2, 4], 3: [2]},
    {8: [0, 1, 2, 3]},
]
ORDER = [
    [0, 1, 2, 5, 3, 9, 4, 6, 7, 8],
    [2, 3, 0, 7, 1, 9, 6, 4, 5, 8],
    [4, 5, 6, 1, 7, 9, 0, 2, 3, 8],
    [6, 7, 4, 3, 5, 9, 2, 0, 1, 8],
    [8, 9, 3, 5, 0, 2, 4, 6, 1, 7],
]
COPY = [{1: [0], 2: [1, 2], 3: [5, 3]}, {1: [2], 2: [3, 0], 3: [7, 1]}, {1: [4], 2: [5, 6], 3: [1, 7]},
        {1: [6], 2: [7, 4], 3: [3, 5]}, {1: [8], 2: [9], 3: [3]}]
NM = 4
NF = 2

SCRATCH = {
    "cws": ("sbuf", [128, 64], "int32"),
    "bk0": ("sbuf", [128, 1024], "bfloat16"),
    "bk1": ("sbuf", [128, 1024], "bfloat16"),
    "xs": ("sbuf", [128, 4 * TC], "bfloat16"),
    "xq": ("sbuf", [128, TC], "float8_e4m3fn_x4"),
    "xsc": ("sbuf", [128, TC], "uint8"),
    "wq": ("sbuf", [128, NB * BC], "float8_e4m3fn_x4"),
    "wsc": ("sbuf", [128, NB * BC], "uint8"),
    "ys": ("sbuf", [128, NB * BC], "float32"),
    "ps": ("psum", [128, 512 * 8], "float32"),
}
for _t in range(4):
    SCRATCH["off%d" % _t] = ("sbuf", [128, 2 * LC], "uint16")
    SCRATCH["lof%d" % _t] = ("sbuf", [128, NF * LC], "uint16")
for _k in range(NM):
    SCRATCH["tmp%d" % _k] = ("sbuf", [128, 4 * BC], "bfloat16")
    SCRATCH["w%d" % _k] = ("sbuf", [128, 4 * BC], "bfloat16")

SEMAPHORES = ["ldc", "ldb0", "ldb1", "ldx", "idx", "lidx", "sg", "vw", "vq", "xqd", "mm", "cps", "cpv", "st", "loc"]
SEMAPHORES += ["arr%d" % _b for _b in range(NB)] + ["larr%d" % _b for _b in range(NB)]


def bits(engs):
    return sum(1 << e for e in engs)


def code_groups(r, batch, T, topo):
    me = T.cores[r]
    dst = SEND[r].get(batch, [])
    near = [d for d in dst if topo.chip(T.cores[d]) == topo.chip(me)]
    far = [d for d in dst if d not in near]
    out, fe = [], []
    if far:
        fe = topo.engines(me, T.cores[far[0]])
        out.append((fe, far))
    if near:
        out.append(([e for e in topo.engines(me, T.cores[near[0]]) if e not in fe], near))
    return out


def rank_program(g, core, T, topo):
    r = T.rank_of(core)
    if r is None:
        return
    S = T.sem
    V, A, P = g.vector, g.scalar, g.tensor
    copy = ActivationFunctionType.Copy
    make, order = MAKE[r], ORDER[r]
    foreign = [b for b in make if b // 2 != r]

    def dst_of(d):
        rid, pid, _se = topo.addr(T.cores[d])
        return DstId(rid=rid, pnc=pid)

    def lists_of(k, t):
        b = make[k]
        if b // 2 == r:
            return T["off%d" % t], (b % 2) * LC
        return T["lof%d" % t], foreign.index(b) * LC

    g.sync.dma_start(T.cws[:], T.cw[:, :]).then_inc(S.ldc, 16)
    A.dma_start(T.bk0[:], T.book[:, 0:1024]).then_inc(S.ldb0, 16)
    g.sync.dma_start(T.bk1[:], T.book[:, 1024:2048]).then_inc(S.ldb1, 16)
    A.dma_start(T.xs[:], T.x[:, :]).then_inc(S.ldx, 16)

    V.wait_ge(S.ldc, 16)
    for h in (1, 0):
        for m in range(2):
            for i in range(2):
                src = (2 * (2 * h + i) + m) * 8
                to = h * LC + m * (LC // 2) + i * 8
                V.tensor_scalar(T.off0[:, to:to + 8], T.cws[:, src:src + 8], 4, None, AluOpType.mult).then_inc(S.idx, 1)
    V.wait_ge(S.idx, 8)
    for t in range(1, 4):
        V.tensor_scalar(T["off%d" % t][:], T.off0[:], t, None, AluOpType.add).then_inc(S.idx, 1)

    loc = 0
    tr = []
    asks = {}
    for d in range(NR):
        for b in MAKE[d]:
            if b // 2 == r and d != r:
                asks.setdefault(b, []).append(d)
    for b in sorted(asks):
        engs = topo.engines(core, T.cores[asks[b][0]])
        at = (b % 2) * LC
        dsts = []
        for d in asks[b]:
            f = [q for q in MAKE[d] if q // 2 != d].index(b)
            dsts.append(T.lof0[:, f * LC:(f + 1) * LC])
        tr.append(RemoteDMATransfer(dst_ids=[dst_of(d) for d in asks[b]], dma_engine_mask=bits(engs),
                                    remote_sem=S["larr%d" % b], srcs=[T.off0[:, at:at + LC]], dsts=dsts))
        loc += len(engs)
    if tr:
        g.wait_ge(S.idx, 4)
        g.remote_dma_fused(tr, local_sem=S.loc)

    def list_engines(b):
        return len(topo.engines(T.cores[b // 2], core))

    where = {}
    ncp = {"s": 0, "v": 0}

    def copy_out(i, eng):
        b, h = order[i // 2], i % 2
        bank = (i % 8) * 512
        to = b * BC + h * TC
        ncp[eng] += 1
        if eng == "s":
            A.wait_ge(S.mm, i + 1)
            A.activation(T.ys[:, to:to + TC], T.ps[:, bank:bank + TC], copy).then_inc(S.cps, 1)
            where[i] = (S.cps, ncp[eng])
        else:
            V.wait_ge(S.mm, i + 1)
            V.tensor_copy(T.ys[:, to:to + TC], T.ps[:, bank:bank + TC]).then_inc(S.cpv, 1)
            where[i] = (S.cpv, ncp[eng])

    def foreign_offsets():
        for b in foreign:
            V.wait_ge(S["larr%d" % b], list_engines(b))
        for t in range(1, 4):
            V.tensor_scalar(T["lof%d" % t][:], T.lof0[:], t, None, AluOpType.add).then_inc(S.lidx, 1)

    done = []
    for k in range(NM):
        far_list = make[k] // 2 != r
        if k == 0:
            A.wait_ge(S.ldb0, 16)
        for t in range(4):
            if far_list:
                if t == 0:
                    A.wait_ge(S["larr%d" % make[k]], list_engines(make[k]))
                elif k == NM - NF:
                    A.wait_ge(S.lidx, t)
            elif k == 0:
                A.wait_ge(S.idx, 8 + t)
            buf, at = lists_of(k, t)
            A.activation(T["tmp%d" % k][:, t * BC:(t + 1) * BC],
                         T.bk0[:, 0:1024].indirect(buf[:, at:at + LC // 2]), copy).then_inc(S.sg, 1)
        for b in COPY[r].get(k, []):
            for h in range(2):
                i = 2 * order.index(b) + h
                copy_out(i, "s")
                done.append(i)

    for k in range(NM):
        for t in range(4):
            if k == 0 and t == 0:
                V.wait_ge(S.idx, 11)
                V.wait_ge(S.ldb1, 16)
            if k == NM - NF and t == 0:
                V.wait_ge(S.lidx, 3)
            V.wait_ge(S.sg, 4 * k + t + 1)
            buf, at = lists_of(k, t)
            V.tensor_tensor(T["w%d" % k][:, t:4 * BC:4],
                            T.bk1[:, 0:1024].indirect(buf[:, at + LC // 2:at + LC]),
                            T["tmp%d" % k][:, t * BC:(t + 1) * BC], AluOpType.add).then_inc(S.vw, 1)
            if k == NM - NF - 1 and t == 2:
                foreign_offsets()
        V.wait_ge(S.vw, 4 * (k + 1))
        c = make[k] * BC
        V.quantize_mx(T.wq[:, c:c + BC], T.wsc[:, c:c + BC], T["w%d" % k][:]).then_inc(S.vq, 1)
        if k == 0:
            V.wait_ge(S.ldx, 16)
            V.quantize_mx(T.xq[:], T.xsc[:], T.xs[:]).then_inc(S.xqd, 1)

    rest = [i for i in range(2 * NB) if i not in done]
    for n, i in enumerate(rest):
        copy_out(i, "sv"[n % 2])

    P.wait_ge(S.xqd, 1)
    for j, b in enumerate(order):
        if b in make:
            P.wait_ge(S.vq, make.index(b) + 1)
        else:
            n = 0
            for s in range(NR):
                if r in SEND[s].get(b, []):
                    n += sum(2 * len(e) for e, dd in code_groups(s, b, T, topo) if r in dd)
            P.wait_ge(S["arr%d" % b], n)
        for h in range(2):
            i = 2 * j + h
            if i >= 8:
                P.wait_ge(where[i - 8][0], where[i - 8][1])
            c = b * BC + h * TC
            bank = (i % 8) * 512
            P.matmul_mx(T.ps[:, bank:bank + TC], T.wq[:, c:c + TC], T.wsc[:, c:c + TC], T.xq[:], T.xsc[:],
                        True, True).then_inc(S.mm, 1)

    for j, b in enumerate(order):
        for h in range(2):
            g.sync.wait_ge(where[2 * j + h][0], where[2 * j + h][1])
        g.sync.dma_start(T.y[:, b * BC:(b + 1) * BC], T.ys[:, b * BC:(b + 1) * BC]).then_inc(S.st, 16)
    g.sync.wait_ge(S.st, 16 * NB)

    for k, b in enumerate(make):
        grp = code_groups(r, b, T, topo)
        if not grp:
            continue
        g.wait_ge(S.vq, k + 1)
        c = b * BC
        for src in (T.wq[:, c:c + BC].bitcast(dt.uint8), T.wsc[:, c:c + BC]):
            tr = []
            for engs, dd in grp:
                tr.append(RemoteDMATransfer(dst_ids=[dst_of(d) for d in dd], dma_engine_mask=bits(engs),
                                            remote_sem=S["arr%d" % b], srcs=[src], dsts=[src] * len(dd)))
                loc += len(engs)
            g.remote_dma_fused(tr, local_sem=S.loc)
    g.wait_ge(S.loc, loc)
